import numpy as np
import ml_dtypes


def mxq(x, axis, fmt="e4m3"):
    dtype, down = {"e4m3": (ml_dtypes.float8_e4m3fn, 7), "e5m2": (ml_dtypes.float8_e5m2, 14)}[fmt]
    v = np.moveaxis(np.asarray(x, np.float32).astype(ml_dtypes.bfloat16).astype(np.float64), axis, -1)
    blocks = v.reshape(v.shape[:-1] + (-1, 32))
    amax = np.abs(blocks).max(-1, keepdims=True)
    byte = np.maximum(np.where(amax > 0, np.frexp(amax)[1] - 1 + 127, 0) - down, 1)
    scale = np.exp2(byte - 127.0)
    codes = (blocks / scale).astype(np.float32).astype(dtype).astype(np.float64)
    return np.moveaxis((codes * scale).reshape(v.shape), -1, axis)


WIDE = False


def mx_kscale(k):
    if not WIDE:
        return np.ones(k)
    levels = np.array([10, -10, 5, -5, 0])
    if k % 512:
        return np.exp2(np.random.permutation(np.resize(levels, k // 32))).repeat(32)
    a = np.empty((k // 512, 16))
    for p in range(k // 512):
        a[p, :8] = np.random.permutation(np.resize(levels, 8))
        for g in range(8):
            far = levels[np.abs(levels - a[p, g]) >= 10]
            a[p, g + 8] = far[np.random.randint(len(far))]
    return np.exp2(a.ravel()).repeat(32)


def f64(x):
    return np.asarray(x).astype(np.float64)


def striped(idx):
    return np.tile(np.asarray(idx).reshape(-1, 16).T, (8, 1)).astype(np.uint16)


def unstriped(offs):
    return offs[:16].T.reshape(-1).astype(np.int64)


B, N, T, D, NQ = 1, 512, 2048, 512, 256
DV = 512


def setup_inputs():
    n = np.random.standard_normal
    idx = np.random.permutation(T)[:B * N]
    u = mx_kscale(N)
    ut = np.ones(T)
    ut[idx] = u
    return {
        "vT": (n((DV, T)) / ut).astype(np.float32),
        "wT": (np.random.dirichlet(np.ones(N), NQ).T[None] * u[:, None] * 16).astype(np.float32),
        "gn": (np.random.uniform(0.5, 2.0, (B, 1, DV))).astype(np.float32),
        "offs": striped(idx),
    }


def reference(vT, wT, gn, offs):
    idx = unstriped(offs)
    pick = lambda x, which: x[:, which].reshape(x.shape[0], B, -1).transpose(1, 0, 2)
    wq = mxq(f64(wT), 1, "e4m3")
    o = wq.transpose(0, 2, 1) @ mxq(pick(f64(vT), idx).transpose(0, 2, 1), 1, "e4m3")
    ms = np.mean(np.square(o), axis=-1, keepdims=True)
    r_ = o / np.sqrt(ms + 1e-05) * f64(gn)
    return r_

@@ -1,0 +1,159 @@
+from contextlib import ExitStack
+
+import concourse.mybir as mybir
+from concourse.masks import make_identity
+
+SLOTS, TOKENS, FEATURES, QUERIES = 512, 2048, 512, 256
+EPS = 1e-05
+FLOPS = 2 * QUERIES * SLOTS * FEATURES
+
+F32 = mybir.dt.float32
+BF16 = mybir.dt.bfloat16
+U32 = mybir.dt.uint32
+U16 = mybir.dt.uint16
+U8 = mybir.dt.uint8
+FP8X4 = mybir.dt.float8_e4m3fn_x4
+ALU = mybir.AluOpType
+ACT = mybir.ActivationFunctionType
+
+P = 128
+PACK = 4
+BLOCKS = FEATURES // P
+Q_TILES = QUERIES // P
+
+
+def tile_attend_wsum_rms_f_topk_kernel(tc, vT, wT, gn, offs, out):
+    nc = tc.nc
+    last = BLOCKS - 1
+    early_cols = slice(0, last * P)
+    last_cols = slice(last * P, FEATURES)
+    with ExitStack() as ctx:
+        keep = ctx.enter_context(tc.tile_pool(name="keep", bufs=1))
+        reuse = ctx.enter_context(tc.tile_pool(name="reuse", bufs=1))
+        stage = ctx.enter_context(tc.tile_pool(name="stage", bufs=2))
+        turn_psum = ctx.enter_context(tc.psum_pool(name="turn_psum", bufs=2))
+        sum_psum = ctx.enter_context(tc.psum_pool(name="sum_psum", bufs=1))
+
+        offsets = keep.tile([P, SLOTS // 16], U16, name="offsets")
+        gain_cols = keep.tile([P, PACK], F32, name="gain_cols")
+        pools = []
+        for b in range(BLOCKS):
+            pool_b = reuse.tile([P, TOKENS], F32, name="pool%d" % b, tag="pool%d" % b, align_bytes=64)
+            nc.sync.dma_start(out=pool_b[:], in_=vT[b * P : (b + 1) * P, :])
+            pools.append(pool_b)
+            if b == 0:
+                nc.sync.dma_start(offsets[:], offs)
+                nc.sync.dma_start(out=gain_cols[:], in_=gn[0, 0].rearrange("(p c) -> p c", c=PACK))
+        w_raw = reuse.tile([P, PACK, QUERIES], F32, name="w_raw", tag="w_raw", align_bytes=64)
+        nc.sync.dma_start(out=w_raw[:], in_=wT[0].rearrange("(p r) q -> p r q", r=PACK))
+
+        ident = keep.tile([P, P], F32, name="ident")
+        make_identity(nc, ident[:])
+
+        warm = keep.tile([P, 1], F32, name="warm")
+        nc.scalar.activation(warm[:], ident[:, 0:1], ACT.Abs_reciprocal_sqrt, bias=1.0)
+
+        gain_turned = turn_psum.tile([P, PACK, P], F32, name="gain_turned", tag="turned")
+        for c in range(PACK):
+            nc.tensor.transpose(gain_turned[:, c, :], gain_cols[:, c : c + 1].to_broadcast([P, P]), ident[:])
+        gain = keep.tile([P, FEATURES], F32, name="gain")
+        nc.scalar.copy(
+            out=gain[:].rearrange("p (n c) -> p n c", c=PACK),
+            in_=gain_turned[:].rearrange("p c n -> p n c"),
+        )
+
+        def gather_and_turn(b):
+            picked = stage.tile([P, SLOTS], BF16, name="picked", align_bytes=64)
+            nc.vector.tensor_copy(
+                picked[:].rearrange("e (u p j) -> e p j u", u=2, j=2),
+                pools[b][:].indirect(offsets[:]),
+            )
+            words = picked[:].bitcast(F32)
+            turned = turn_psum.tile([P, 2, P], F32, name="turned", tag="turned")
+            for u in range(2):
+                nc.tensor.transpose(turned[:, u, :], words[:, u * P : (u + 1) * P], ident[:])
+            return turned
+
+        def interleave_values(copy, turned, v_grouped):
+            copy(
+                out=v_grouped[:].bitcast(F32).rearrange("p (e u) -> p e u", u=2),
+                in_=turned[:].rearrange("p u e -> p e u"),
+            )
+
+        def quantise(grouped, codes, name):
+            scales = keep.tile([P, P], U8, name=name, align_bytes=64)
+            nc.vector.quantize_mx(out=codes[:].bitcast(FP8X4), scales=scales[:], in_=grouped[:])
+            return codes, scales
+
+        values = []
+        turned = gather_and_turn(0)
+        for b in range(last):
+            v_grouped = stage.tile([P, P * PACK], BF16, name="v_grouped", align_bytes=64)
+            interleave_values(nc.scalar.copy, turned, v_grouped)
+            turned = gather_and_turn(b + 1)
+            v_codes = reuse.tile([P, P], U32, name="v_codes%d" % b, tag="pool%d" % (b + 1), align_bytes=64)
+            values.append(quantise(v_grouped, v_codes, "v_scales%d" % b))
+
+        weights = []
+        w_groups = []
+        for q in range(Q_TILES):
+            w_grouped = keep.tile([P, P * PACK], BF16, name="w_grouped%d" % q, align_bytes=64)
+            copy = nc.vector.tensor_copy if q == 0 else nc.scalar.copy
+            copy(
+                out=w_grouped[:].rearrange("p (q u j) -> p q u j", u=2, j=2),
+                in_=w_raw[:, :, q * P : (q + 1) * P].rearrange("p (j u) q -> p q u j", u=2),
+            )
+            w_groups.append(w_grouped)
+        for q in range(Q_TILES):
+            w_codes = keep.tile([P, P], U32, name="w_codes%d" % q, align_bytes=64)
+            weights.append(quantise(w_groups[q], w_codes, "w_scales%d" % q))
+
+        last_grouped = reuse.tile([P, P * PACK], BF16, name="last_grouped", tag="w_raw", align_bytes=64)
+        interleave_values(nc.vector.tensor_copy, turned, last_grouped)
+        last_codes = keep.tile([P, P], U32, name="last_codes", align_bytes=64)
+        values.append(quantise(last_grouped, last_codes, "last_scales"))
+
+        def multiply(sums, q, b):
+            nc.tensor.matmul_mx(
+                out=sums,
+                lhsT=weights[q][0][:].bitcast(FP8X4),
+                lhsT_scale=weights[q][1][:],
+                rhs=values[b][0][:].bitcast(FP8X4),
+                rhs_scale=values[b][1][:],
+                start=True,
+                stop=True,
+            )
+
+        gained = reuse.tile([P, Q_TILES, FEATURES], F32, name="gained", tag="w_raw", align_bytes=64)
+        early_means = []
+        for q in range(Q_TILES):
+            early_sums = sum_psum.tile([P, last * P], F32, name="early_sums%d" % q)
+            for b in range(last):
+                multiply(early_sums[:, b * P : (b + 1) * P], q, b)
+            early_squared = stage.tile([P, last * P], F32, name="early_squared")
+            early_squares = stage.tile([P, 1], F32, name="early_squares")
+            nc.scalar.activation(early_squared[:], early_sums[:], ACT.Square, accum_out=early_squares[:])
+            nc.vector.tensor_tensor(gained[:, q, early_cols], early_sums[:], gain[:, early_cols], ALU.mult)
+            early_mean = stage.tile([P, 1], F32, name="early_mean")
+            nc.scalar.activation(early_mean[:], early_squares[:], ACT.Copy, bias=EPS, scale=1.0 / FEATURES)
+            early_means.append(early_mean)
+
+        last_squares = []
+        for q in range(Q_TILES):
+            last_sums = sum_psum.tile([P, P], F32, name="last_sums%d" % q)
+            multiply(last_sums[:], q, last)
+            last_squared = stage.tile([P, P], F32, name="last_squared")
+            squares = stage.tile([P, 1], F32, name="squares")
+            nc.scalar.activation(last_squared[:], last_sums[:], ACT.Square, accum_out=squares[:])
+            nc.vector.tensor_tensor(gained[:, q, last_cols], last_sums[:], gain[:, last_cols], ALU.mult)
+            last_squares.append(squares)
+
+        for q in range(Q_TILES):
+            inv_rms = stage.tile([P, 1], F32, name="inv_rms")
+            nc.scalar.activation(
+                inv_rms[:], last_squares[q][:], ACT.Abs_reciprocal_sqrt,
+                bias=early_means[q][:], scale=1.0 / FEATURES,
+            )
+            result = stage.tile([P, FEATURES], F32, name="result")
+            nc.vector.tensor_scalar(result[:], gained[:, q, :], inv_rms[:], None, ALU.mult)
+            nc.sync.dma_start(out=out[0, q * P : (q + 1) * P, :], in_=result[:])

@@ -1,3 +1,4 @@
+import math
 from contextlib import ExitStack
 
 import concourse.mybir as mybir
@@ -44,14 +45,27 @@ def tile_attend_wsum_rms_f_topk_kernel(tc, vT, wT, gn, offs, out):
             if b == 0:
                 nc.sync.dma_start(offsets[:], offs)
                 nc.sync.dma_start(out=gain_cols[:], in_=gn[0, 0].rearrange("(p c) -> p c", c=PACK))
-        w_raw = reuse.tile([P, PACK, QUERIES], F32, name="w_raw", tag="w_raw", align_bytes=64)
-        nc.sync.dma_start(out=w_raw[:], in_=wT[0].rearrange("(p r) q -> p r q", r=PACK))
+        w_raws = []
+        for q in range(Q_TILES):
+            w_raw = reuse.tile([P, PACK, P], F32, name="w_raw%d" % q, tag="w_raw%d" % q, align_bytes=64)
+            nc.sync.dma_start(out=w_raw[:], in_=wT[0, :, q * P : (q + 1) * P].rearrange("(p r) q -> p r q", r=PACK))
+            w_raws.append(w_raw)
 
         ident = keep.tile([P, P], F32, name="ident")
         make_identity(nc, ident[:])
 
-        warm = keep.tile([P, 1], F32, name="warm")
-        nc.scalar.activation(warm[:], ident[:, 0:1], ACT.Abs_reciprocal_sqrt, bias=1.0)
+        count = keep.tile([P, 1], F32, name="count")
+        nc.gpsimd.memset(count[:], float(FEATURES))
+        inv_root = keep.tile([P, 1], F32, name="inv_root")
+        nc.scalar.activation(inv_root[:], count[:], ACT.Abs_reciprocal_sqrt)
+
+        root_eps = keep.tile([P, 1], F32, name="root_eps")
+        nc.vector.tensor_scalar(root_eps[:], count[:], math.sqrt(EPS / FEATURES), None, ALU.mult)
+        early_banks = []
+        for q in range(Q_TILES):
+            early_sums = sum_psum.tile([P, FEATURES], F32, name="early_sums%d" % q)
+            nc.tensor.transpose(early_sums[:, last_cols], root_eps[:].to_broadcast([P, P]), ident[:])
+            early_banks.append(early_sums)
 
         gain_turned = turn_psum.tile([P, PACK, P], F32, name="gain_turned", tag="turned")
         for c in range(PACK):
@@ -98,17 +112,16 @@ def tile_attend_wsum_rms_f_topk_kernel(tc, vT, wT, gn, offs, out):
         w_groups = []
         for q in range(Q_TILES):
             w_grouped = keep.tile([P, P * PACK], BF16, name="w_grouped%d" % q, align_bytes=64)
-            copy = nc.vector.tensor_copy if q == 0 else nc.scalar.copy
-            copy(
+            nc.scalar.copy(
                 out=w_grouped[:].rearrange("p (q u j) -> p q u j", u=2, j=2),
-                in_=w_raw[:, :, q * P : (q + 1) * P].rearrange("p (j u) q -> p q u j", u=2),
+                in_=w_raws[q][:].rearrange("p (j u) q -> p q u j", u=2),
             )
             w_groups.append(w_grouped)
         for q in range(Q_TILES):
             w_codes = keep.tile([P, P], U32, name="w_codes%d" % q, align_bytes=64)
             weights.append(quantise(w_groups[q], w_codes, "w_scales%d" % q))
 
-        last_grouped = reuse.tile([P, P * PACK], BF16, name="last_grouped", tag="w_raw", align_bytes=64)
+        last_grouped = reuse.tile([P, P * PACK], BF16, name="last_grouped", tag="w_raw1", align_bytes=64)
         interleave_values(nc.vector.tensor_copy, turned, last_grouped)
         last_codes = keep.tile([P, P], U32, name="last_codes", align_bytes=64)
         values.append(quantise(last_grouped, last_codes, "last_scales"))
@@ -124,29 +137,36 @@ def tile_attend_wsum_rms_f_topk_kernel(tc, vT, wT, gn, offs, out):
                 stop=True,
             )
 
-        gained = reuse.tile([P, Q_TILES, FEATURES], F32, name="gained", tag="w_raw", align_bytes=64)
+        gained = reuse.tile([P, Q_TILES, last * P], F32, name="gained", tag="w_raw1", align_bytes=64)
         early_means = []
         for q in range(Q_TILES):
-            early_sums = sum_psum.tile([P, last * P], F32, name="early_sums%d" % q)
+            early_sums = early_banks[q]
             for b in range(last):
                 multiply(early_sums[:, b * P : (b + 1) * P], q, b)
-            early_squared = stage.tile([P, last * P], F32, name="early_squared")
-            early_squares = stage.tile([P, 1], F32, name="early_squares")
-            nc.scalar.activation(early_squared[:], early_sums[:], ACT.Square, accum_out=early_squares[:])
-            nc.vector.tensor_tensor(gained[:, q, early_cols], early_sums[:], gain[:, early_cols], ALU.mult)
+            early_squared = stage.tile([P, last * P + 1], F32, name="early_squared")
             early_mean = stage.tile([P, 1], F32, name="early_mean")
-            nc.scalar.activation(early_mean[:], early_squares[:], ACT.Copy, bias=EPS, scale=1.0 / FEATURES)
+            nc.scalar.activation(
+                early_squared[:], early_sums[:, 0 : last * P + 1], ACT.Square, scale=inv_root[:], accum_out=early_mean[:]
+            )
             early_means.append(early_mean)
+            nc.vector.tensor_tensor(gained[:, q, :], early_sums[:, early_cols], gain[:, early_cols], ALU.mult)
 
         last_squares = []
+        last_banks = []
         for q in range(Q_TILES):
             last_sums = sum_psum.tile([P, P], F32, name="last_sums%d" % q)
             multiply(last_sums[:], q, last)
             last_squared = stage.tile([P, P], F32, name="last_squared")
             squares = stage.tile([P, 1], F32, name="squares")
             nc.scalar.activation(last_squared[:], last_sums[:], ACT.Square, accum_out=squares[:])
-            nc.vector.tensor_tensor(gained[:, q, last_cols], last_sums[:], gain[:, last_cols], ALU.mult)
             last_squares.append(squares)
+            last_banks.append(last_sums)
+
+        def scale_gained(q, result, source, factor):
+            if q == 0:
+                nc.vector.tensor_scalar(result, source, factor, None, ALU.mult)
+            else:
+                nc.scalar.activation(result, source, ACT.Copy, scale=factor)
 
         for q in range(Q_TILES):
             inv_rms = stage.tile([P, 1], F32, name="inv_rms")
@@ -154,6 +174,14 @@ def tile_attend_wsum_rms_f_topk_kernel(tc, vT, wT, gn, offs, out):
                 inv_rms[:], last_squares[q][:], ACT.Abs_reciprocal_sqrt,
                 bias=early_means[q][:], scale=1.0 / FEATURES,
             )
-            result = stage.tile([P, FEATURES], F32, name="result")
-            nc.vector.tensor_scalar(result[:], gained[:, q, :], inv_rms[:], None, ALU.mult)
-            nc.sync.dma_start(out=out[0, q * P : (q + 1) * P, :], in_=result[:])
+            half = FEATURES // 2
+            rows = slice(q * P, (q + 1) * P)
+            low = keep.tile([P, half], F32, name="low%d" % q)
+            scale_gained(q, low[:], gained[:, q, 0:half], inv_rms[:])
+            nc.sync.dma_start(out=out[0, rows, 0:half], in_=low[:])
+            high = keep.tile([P, half], F32, name="high%d" % q)
+            scale_gained(q, high[:, 0:P], gained[:, q, half : last * P], inv_rms[:])
+            nc.vector.scalar_tensor_tensor(
+                high[:, P:half], last_banks[q][:], inv_rms[:], gain[:, last_cols], ALU.mult, ALU.mult
+            )
+            nc.sync.dma_start(out=out[0, rows, half:FEATURES], in_=high[:])

import math
from contextlib import ExitStack

import concourse.mybir as mybir
from concourse.masks import make_identity

SLOTS, TOKENS, FEATURES, QUERIES = 512, 2048, 512, 256
EPS = 1e-05
FLOPS = 2 * QUERIES * SLOTS * FEATURES

F32 = mybir.dt.float32
BF16 = mybir.dt.bfloat16
U32 = mybir.dt.uint32
U16 = mybir.dt.uint16
U8 = mybir.dt.uint8
FP8X4 = mybir.dt.float8_e4m3fn_x4
ALU = mybir.AluOpType
ACT = mybir.ActivationFunctionType

P = 128
PACK = 4
BLOCKS = FEATURES // P
Q_TILES = QUERIES // P


def tile_attend_wsum_rms_f_topk_kernel(tc, vT, wT, gn, offs, out):
    nc = tc.nc
    last = BLOCKS - 1
    early_cols = slice(0, last * P)
    last_cols = slice(last * P, FEATURES)
    with ExitStack() as ctx:
        keep = ctx.enter_context(tc.tile_pool(name="keep", bufs=1))
        reuse = ctx.enter_context(tc.tile_pool(name="reuse", bufs=1))
        stage = ctx.enter_context(tc.tile_pool(name="stage", bufs=2))
        turn_psum = ctx.enter_context(tc.psum_pool(name="turn_psum", bufs=2))
        sum_psum = ctx.enter_context(tc.psum_pool(name="sum_psum", bufs=1))

        offsets = keep.tile([P, SLOTS // 16], U16, name="offsets")
        gain_cols = keep.tile([P, PACK], F32, name="gain_cols")
        pools = []
        for b in range(BLOCKS):
            pool_b = reuse.tile([P, TOKENS], F32, name="pool%d" % b, tag="pool%d" % b, align_bytes=64)
            nc.sync.dma_start(out=pool_b[:], in_=vT[b * P : (b + 1) * P, :])
            pools.append(pool_b)
            if b == 0:
                nc.sync.dma_start(offsets[:], offs)
                nc.sync.dma_start(out=gain_cols[:], in_=gn[0, 0].rearrange("(p c) -> p c", c=PACK))
        w_raws = []
        for q in range(Q_TILES):
            w_raw = reuse.tile([P, PACK, P], F32, name="w_raw%d" % q, tag="w_raw%d" % q, align_bytes=64)
            nc.sync.dma_start(out=w_raw[:], in_=wT[0, :, q * P : (q + 1) * P].rearrange("(p r) q -> p r q", r=PACK))
            w_raws.append(w_raw)

        ident = keep.tile([P, P], F32, name="ident")
        make_identity(nc, ident[:])

        count = keep.tile([P, 1], F32, name="count")
        nc.gpsimd.memset(count[:], float(FEATURES))
        inv_root = keep.tile([P, 1], F32, name="inv_root")
        nc.scalar.activation(inv_root[:], count[:], ACT.Abs_reciprocal_sqrt)

        root_eps = keep.tile([P, 1], F32, name="root_eps")
        nc.vector.tensor_scalar(root_eps[:], count[:], math.sqrt(EPS / FEATURES), None, ALU.mult)
        early_banks = []
        for q in range(Q_TILES):
            early_sums = sum_psum.tile([P, FEATURES], F32, name="early_sums%d" % q)
            nc.tensor.transpose(early_sums[:, last_cols], root_eps[:].to_broadcast([P, P]), ident[:])
            early_banks.append(early_sums)

        gain_turned = turn_psum.tile([P, PACK, P], F32, name="gain_turned", tag="turned")
        for c in range(PACK):
            nc.tensor.transpose(gain_turned[:, c, :], gain_cols[:, c : c + 1].to_broadcast([P, P]), ident[:])
        gain = keep.tile([P, FEATURES], F32, name="gain")
        nc.scalar.copy(
            out=gain[:].rearrange("p (n c) -> p n c", c=PACK),
            in_=gain_turned[:].rearrange("p c n -> p n c"),
        )

        def gather_and_turn(b):
            picked = stage.tile([P, SLOTS], BF16, name="picked", align_bytes=64)
            nc.vector.tensor_copy(
                picked[:].rearrange("e (u p j) -> e p j u", u=2, j=2),
                pools[b][:].indirect(offsets[:]),
            )
            words = picked[:].bitcast(F32)
            turned = turn_psum.tile([P, 2, P], F32, name="turned", tag="turned")
            for u in range(2):
                nc.tensor.transpose(turned[:, u, :], words[:, u * P : (u + 1) * P], ident[:])
            return turned

        def interleave_values(copy, turned, v_grouped):
            copy(
                out=v_grouped[:].bitcast(F32).rearrange("p (e u) -> p e u", u=2),
                in_=turned[:].rearrange("p u e -> p e u"),
            )

        def quantise(grouped, codes, name):
            scales = keep.tile([P, P], U8, name=name, align_bytes=64)
            nc.vector.quantize_mx(out=codes[:].bitcast(FP8X4), scales=scales[:], in_=grouped[:])
            return codes, scales

        values = []
        turned = gather_and_turn(0)
        for b in range(last):
            v_grouped = stage.tile([P, P * PACK], BF16, name="v_grouped", align_bytes=64)
            interleave_values(nc.scalar.copy, turned, v_grouped)
            turned = gather_and_turn(b + 1)
            v_codes = reuse.tile([P, P], U32, name="v_codes%d" % b, tag="pool%d" % (b + 1), align_bytes=64)
            values.append(quantise(v_grouped, v_codes, "v_scales%d" % b))

        weights = []
        w_groups = []
        for q in range(Q_TILES):
            w_grouped = keep.tile([P, P * PACK], BF16, name="w_grouped%d" % q, align_bytes=64)
            nc.scalar.copy(
                out=w_grouped[:].rearrange("p (q u j) -> p q u j", u=2, j=2),
                in_=w_raws[q][:].rearrange("p (j u) q -> p q u j", u=2),
            )
            w_groups.append(w_grouped)
        for q in range(Q_TILES):
            w_codes = keep.tile([P, P], U32, name="w_codes%d" % q, align_bytes=64)
            weights.append(quantise(w_groups[q], w_codes, "w_scales%d" % q))

        last_grouped = reuse.tile([P, P * PACK], BF16, name="last_grouped", tag="w_raw1", align_bytes=64)
        interleave_values(nc.vector.tensor_copy, turned, last_grouped)
        last_codes = keep.tile([P, P], U32, name="last_codes", align_bytes=64)
        values.append(quantise(last_grouped, last_codes, "last_scales"))

        def multiply(sums, q, b):
            nc.tensor.matmul_mx(
                out=sums,
                lhsT=weights[q][0][:].bitcast(FP8X4),
                lhsT_scale=weights[q][1][:],
                rhs=values[b][0][:].bitcast(FP8X4),
                rhs_scale=values[b][1][:],
                start=True,
                stop=True,
            )

        gained = reuse.tile([P, Q_TILES, last * P], F32, name="gained", tag="w_raw1", align_bytes=64)
        early_means = []
        for q in range(Q_TILES):
            early_sums = early_banks[q]
            for b in range(last):
                multiply(early_sums[:, b * P : (b + 1) * P], q, b)
            early_squared = stage.tile([P, last * P + 1], F32, name="early_squared")
            early_mean = stage.tile([P, 1], F32, name="early_mean")
            nc.scalar.activation(
                early_squared[:], early_sums[:, 0 : last * P + 1], ACT.Square, scale=inv_root[:], accum_out=early_mean[:]
            )
            early_means.append(early_mean)
            nc.vector.tensor_tensor(gained[:, q, :], early_sums[:, early_cols], gain[:, early_cols], ALU.mult)

        last_squares = []
        last_banks = []
        for q in range(Q_TILES):
            last_sums = sum_psum.tile([P, P], F32, name="last_sums%d" % q)
            multiply(last_sums[:], q, last)
            last_squared = stage.tile([P, P], F32, name="last_squared")
            squares = stage.tile([P, 1], F32, name="squares")
            nc.scalar.activation(last_squared[:], last_sums[:], ACT.Square, accum_out=squares[:])
            last_squares.append(squares)
            last_banks.append(last_sums)

        def scale_gained(q, result, source, factor):
            if q == 0:
                nc.vector.tensor_scalar(result, source, factor, None, ALU.mult)
            else:
                nc.scalar.activation(result, source, ACT.Copy, scale=factor)

        for q in range(Q_TILES):
            inv_rms = stage.tile([P, 1], F32, name="inv_rms")
            nc.scalar.activation(
                inv_rms[:], last_squares[q][:], ACT.Abs_reciprocal_sqrt,
                bias=early_means[q][:], scale=1.0 / FEATURES,
            )
            half = FEATURES // 2
            rows = slice(q * P, (q + 1) * P)
            low = keep.tile([P, half], F32, name="low%d" % q)
            scale_gained(q, low[:], gained[:, q, 0:half], inv_rms[:])
            nc.sync.dma_start(out=out[0, rows, 0:half], in_=low[:])
            high = keep.tile([P, half], F32, name="high%d" % q)
            scale_gained(q, high[:, 0:P], gained[:, q, half : last * P], inv_rms[:])
            nc.vector.scalar_tensor_tensor(
                high[:, P:half], last_banks[q][:], inv_rms[:], gain[:, last_cols], ALU.mult, ALU.mult
            )
            nc.sync.dma_start(out=out[0, rows, half:FEATURES], in_=high[:])
